import numpy as np
import ml_dtypes


def mxq(x, axis, fmt="e4m3"):
    dtype, down = {"e4m3": (ml_dtypes.float8_e4m3fn, 7), "e5m2": (ml_dtypes.float8_e5m2, 14)}[fmt]
    v = np.moveaxis(np.asarray(x, np.float32).astype(ml_dtypes.bfloat16).astype(np.float64), axis, -1)
    blocks = v.reshape(v.shape[:-1] + (-1, 32))
    amax = np.abs(blocks).max(-1, keepdims=True)
    byte = np.maximum(np.where(amax > 0, np.frexp(amax)[1] - 1 + 127, 0) - down, 1)
    scale = np.exp2(byte - 127.0)
    codes = (blocks / scale).astype(np.float32).astype(dtype).astype(np.float64)
    return np.moveaxis((codes * scale).reshape(v.shape), -1, axis)


WIDE = False


def mx_kscale(k):
    if not WIDE:
        return np.ones(k)
    levels = np.array([10, -10, 5, -5, 0])
    if k % 512:
        return np.exp2(np.random.permutation(np.resize(levels, k // 32))).repeat(32)
    a = np.empty((k // 512, 16))
    for p in range(k // 512):
        a[p, :8] = np.random.permutation(np.resize(levels, 8))
        for g in range(8):
            far = levels[np.abs(levels - a[p, g]) >= 10]
            a[p, g + 8] = far[np.random.randint(len(far))]
    return np.exp2(a.ravel()).repeat(32)


def f64(x):
    return np.asarray(x).astype(np.float64)


def striped8(idx):
    return np.concatenate([v.reshape(-1, 16).T for v in idx]).astype(np.uint16)


def unstriped8(offs):
    return np.stack([offs[16 * g:16 * g + 16].T.reshape(-1) for g in range(8)]).astype(np.int64)


E2M1 = np.array([0.0, 0.5, 1.0, 1.5, 2.0, 3.0, 4.0, 6.0, -0.0, -0.5, -1.0, -1.5, -2.0, -3.0, -4.0, -6.0])


def pack_weight(w, fmt):
    k, n = w.shape
    w = f64(np.asarray(w, np.float32).astype(ml_dtypes.bfloat16)).reshape(k // 32, 32, n)
    amax = np.abs(w).max(1)
    if fmt == "e4m3":
        byte = np.frexp(amax)[1] - 1 + 127 - 7
    else:
        mant, ex = np.frexp(amax / 6.0)
        byte = np.where(mant > 0.5, ex, ex - 1) + 127
    byte = np.clip(np.where(amax > 0, byte, 1), 1, 254)
    scaled = (w * np.exp2(127.0 - byte)[:, None, :]).reshape(k, n).astype(np.float32)
    by_word = np.ascontiguousarray(scaled.reshape(k // 512, 128, 4, n).transpose(0, 1, 3, 2))
    if fmt == "e4m3":
        words = by_word.astype(ml_dtypes.float8_e4m3fn).view(np.uint8)
    else:
        c = by_word.astype(ml_dtypes.float4_e2m1fn).view(np.uint8) & 0xF
        words = (c[..., 0::2] | (c[..., 1::2] << 4)).reshape(k // 512, 128, 2 * n)
    return np.ascontiguousarray(words), np.ascontiguousarray(byte.astype(np.uint8).reshape(k // 512, 16, n))


def unpack_weight(words, scales, fmt):
    g, _, n = scales.shape
    words = np.ascontiguousarray(words).reshape(g, 128, n, -1)
    if fmt == "e4m3":
        vals = words.view(ml_dtypes.float8_e4m3fn).astype(np.float64)
    else:
        nib = np.empty((g, 128, n, 4), np.uint8)
        nib[..., 0::2] = words & 0xF
        nib[..., 1::2] = words >> 4
        vals = E2M1[nib]
    vals = vals * np.repeat(np.exp2(scales.astype(np.float64) - 127.0), 8, axis=1)[..., None]
    return vals.transpose(0, 1, 3, 2).reshape(g * 512, n)


G, K, M, T, S = 2, 512, 1024, 1024, 256


def setup_inputs():
    n = np.random.standard_normal
    s = mx_kscale(K)[:, None]
    p_w = pack_weight(n((K, M)) / np.sqrt(K) / s, "e2m1")
    return {
        "xT": (n((K, T)) * s).astype(np.float32),
        "w_words": p_w[0],
        "w_scales": p_w[1],
        "wgt": np.repeat(np.random.uniform(0.5, 2.0, (8, G * S)), 16, axis=0).astype(np.float32),
        "b": (0.3 * n(1024)).astype(np.float32),
        "offs": striped8(np.stack([np.concatenate([np.random.permutation(T)[:S] for _ in range(G)]) for _ in range(8)])),
    }


def reference(xT, w_words, w_scales, wgt, b, offs):
    idx = unstriped8(offs)
    group = np.arange(K) % 512 // 64
    xg = f64(wgt)[np.arange(K) // 4 % 128] * f64(xT)[np.arange(K)[:, None], idx[group]]
    xT_ = mxq(xg, 0, "e4m3")
    xT_ = xT_.reshape(K, G, S).sum(1)
    w_ = unpack_weight(w_words, w_scales, "e2m1")
    y = xT_.T @ w_
    return y + f64(b)[None, :]

@@ -1,0 +1,153 @@
+from contextlib import ExitStack
+
+import concourse.mybir as mybir
+from concourse.masks import make_identity
+
+G, K, M, T, S = 2, 512, 1024, 1024, 256
+FLOPS = 2 * G * K * S * M
+
+F32 = mybir.dt.float32
+BF16 = mybir.dt.bfloat16
+I32 = mybir.dt.int32
+U32 = mybir.dt.uint32
+U16 = mybir.dt.uint16
+U8 = mybir.dt.uint8
+FP8X4 = mybir.dt.float8_e4m3fn_x4
+FP4X4 = mybir.dt.float4_e2m1fn_x4
+MULT = mybir.AluOpType.mult
+ADD = mybir.AluOpType.add
+
+P = 128
+PACK = 4
+CH = 128
+NT = 512
+
+
+def tile_list_hbag_tm_bias_kernel(tc, xT, w_words, w_scales, wgt, b, offs, out):
+    nc = tc.nc
+    with ExitStack() as ctx:
+        keep = ctx.enter_context(tc.tile_pool(name="keep", bufs=1))
+        psum = ctx.enter_context(tc.psum_pool(name="psum", bufs=1))
+
+        offsets = keep.tile([P, G * S // 16], U16, name="offsets")
+        planes = [keep.tile([P, T], F32, name=f"plane{i}") for i in range(PACK)]
+        arena = keep.tile([P, 9, CH], F32, name="arena")
+        words = keep.tile([P, 2 * M], U8, name="words", align_bytes=64)
+        wsc = keep.tile([P, M], U8, name="wsc", align_bytes=64)
+        bcol = keep.tile([P, M // P], F32, name="bcol", tag="woven1", align_bytes=64)
+        ident = keep.tile([P, P], F32, name="ident", tag="woven0", align_bytes=64)
+        bias = keep.tile([P, M], F32, name="bias")
+
+        x_planes = xT.rearrange("(p i) t -> p i t", i=PACK)
+        nc.sync.dma_start(out=bcol[:], in_=b.rearrange("(p c) -> p c", p=P))
+        nc.vector.memset(wsc[:].bitcast(I32), 0)
+        make_identity(nc, ident[:])
+
+        nc.sync.dma_start(out=planes[0][:], in_=x_planes[:, 0, :])
+        nc.sync.dma_start(offsets[:], offs)
+        wgt_q = wgt.rearrange("p (q c) -> p q c", c=CH)
+        for c in range(G):
+            nc.sync.dma_start(out=arena[:, 2 * c : 2 * c + 2, :], in_=wgt_q[:, 2 * c : 2 * c + 2, :])
+        for i in range(1, PACK):
+            nc.sync.dma_start(out=planes[i][:], in_=x_planes[:, i, :])
+        for q in range(4):
+            nc.sync.dma_start(out=wsc[32 * q : 32 * q + 4, :].bitcast(I32), in_=w_scales[0, 4 * q : 4 * q + 4, :].bitcast(I32))
+        nc.sync.dma_start(out=words[:].bitcast(I32), in_=w_words[0].bitcast(I32))
+
+        bias_v = bias[:].rearrange("p (n h c) -> p h n c", h=2, c=4)
+        for h in range(2):
+            spread = psum.tile([P, 4, P], F32, name=f"spread{h}")
+            for c in range(4):
+                nc.tensor.transpose(spread[:, c, :], bcol[:, 4 * h + c : 4 * h + c + 1].to_broadcast([P, P]), ident[:])
+            nc.scalar.copy(out=bias_v[:, h], in_=spread[:].rearrange("p c n -> p n c"))
+
+        low = keep.tile([P, 2, G * S], F32, name="low")
+        woven = {}
+        codes = {q: keep.tile([P, CH], U32, name=f"codes{q}", align_bytes=64) for q in range(4)}
+        scales = {q: keep.tile([P, CH], U8, name=f"scales{q}", align_bytes=64) for q in range(4)}
+        slots = {0: (6, 7), 1: (4, 6), 2: (5, 8), 3: (0, 5)}
+
+        def gather(i, q, count=1):
+            first = slots[q][i - 2]
+            nc.vector.tensor_tensor(
+                arena[:, first : first + count, :].rearrange("p q c -> p (q c)"),
+                planes[i][:].indirect(offsets[:, q * (CH // 16) : (q + count) * (CH // 16)]),
+                arena[:, q : q + count, :].rearrange("p q c -> p (q c)"),
+                MULT,
+            )
+
+        def weave_low(q):
+            woven[q] = keep.tile([P, CH, PACK], BF16, name=f"woven{q}", tag=f"woven{q // 2}", align_bytes=64)
+            nc.scalar.copy(out=woven[q][:, :, 0:2], in_=low[:, :, q * CH : (q + 1) * CH].rearrange("p t c -> p c t"))
+
+        def weave_high(q):
+            s2, s3 = slots[q]
+            nc.scalar.copy(out=woven[q][:, :, 2:4], in_=arena[:, s2 : s3 + 1 : s3 - s2, :].rearrange("p t c -> p c t"))
+
+        def quantise(q):
+            nc.vector.quantize_mx(
+                out=codes[q][:].bitcast(FP8X4),
+                scales=scales[q][:],
+                in_=woven[q][:].rearrange("p c t -> p (c t)"),
+            )
+
+        half = G * S // 2
+        for c in range(G):
+            nc.vector.tensor_tensor(
+                low[:, 0, c * half : (c + 1) * half],
+                planes[0][:].indirect(offsets[:, c * half // 16 : (c + 1) * half // 16]),
+                arena[:, 2 * c : 2 * c + 2, :].rearrange("p q c -> p (q c)"),
+                MULT,
+            )
+        nc.vector.tensor_tensor(low[:, 1, :], planes[1][:].indirect(offsets[:]), arena[:, 0:4, :].rearrange("p q c -> p (q c)"), MULT)
+        weave_low(0)
+        weave_low(2)
+        gather(2, 0)
+        gather(2, 1, 2)
+        gather(3, 0)
+        gather(3, 2)
+        gather(2, 3)
+        weave_high(0)
+        quantise(0)
+        weave_high(2)
+        gather(3, 1)
+        quantise(2)
+        gather(3, 3)
+        weave_low(1)
+        weave_high(1)
+        quantise(1)
+        weave_low(3)
+        weave_high(3)
+        quantise(3)
+
+        def product(acc, h, c, n0, width):
+            q = c * (S // CH) + h
+            nc.tensor.matmul_mx(
+                out=acc,
+                lhsT=codes[q][:].bitcast(FP8X4),
+                lhsT_scale=scales[q][:],
+                rhs=words[:, 2 * n0 : 2 * (n0 + width)].bitcast(FP4X4),
+                rhs_scale=wsc[:, n0 : n0 + width],
+                start=(c == 0),
+                stop=(c == G - 1),
+            )
+
+        def finish(acc, h, n0, width, queue):
+            res = keep.tile([P, width], F32, name=f"res{h}_{n0}")
+            nc.vector.tensor_tensor(res[:], acc[:], bias[:, n0 : n0 + width], ADD)
+            queue.dma_start(out=out[h * CH : (h + 1) * CH, n0 : n0 + width], in_=res[:])
+
+        first = [psum.tile([P, NT], F32, name=f"first{n}") for n in range(2)]
+        for c in range(G):
+            for n in range(M // NT):
+                product(first[n][:], 0, c, n * NT, NT)
+        for n in range(M // NT):
+            finish(first[n], 0, n * NT, NT, nc.sync)
+        n0 = 0
+        for width, step, queue in ((512, 512, nc.sync), (256, 128, nc.sync), (128, 128, nc.scalar), (128, 128, nc.sync)):
+            acc = psum.tile([P, width], F32, name=f"second{n0}")
+            for a in range(0, width, step):
+                for c in range(G):
+                    product(acc[:, a : a + step], 1, c, n0 + a, step)
+            finish(acc, 1, n0, width, queue)
+            n0 = n0 + width

@@ -31,23 +31,22 @@ def tile_list_hbag_tm_bias_kernel(tc, xT, w_words, w_scales, wgt, b, offs, out):
 
         offsets = keep.tile([P, G * S // 16], U16, name="offsets")
         planes = [keep.tile([P, T], F32, name=f"plane{i}") for i in range(PACK)]
-        arena = keep.tile([P, 9, CH], F32, name="arena")
+        weight = keep.tile([P, G * S], F32, name="weight")
         words = keep.tile([P, 2 * M], U8, name="words", align_bytes=64)
         wsc = keep.tile([P, M], U8, name="wsc", align_bytes=64)
-        bcol = keep.tile([P, M // P], F32, name="bcol", tag="woven1", align_bytes=64)
+        bcol = keep.tile([P, M // P], F32, name="bcol")
         ident = keep.tile([P, P], F32, name="ident", tag="woven0", align_bytes=64)
         bias = keep.tile([P, M], F32, name="bias")
 
         x_planes = xT.rearrange("(p i) t -> p i t", i=PACK)
-        nc.sync.dma_start(out=bcol[:], in_=b.rearrange("(p c) -> p c", p=P))
+        nc.scalar.dma_start(out=bcol[:], in_=b.rearrange("(p c) -> p c", p=P))
         nc.vector.memset(wsc[:].bitcast(I32), 0)
         make_identity(nc, ident[:])
 
         nc.sync.dma_start(out=planes[0][:], in_=x_planes[:, 0, :])
         nc.sync.dma_start(offsets[:], offs)
-        wgt_q = wgt.rearrange("p (q c) -> p q c", c=CH)
         for c in range(G):
-            nc.sync.dma_start(out=arena[:, 2 * c : 2 * c + 2, :], in_=wgt_q[:, 2 * c : 2 * c + 2, :])
+            nc.sync.dma_start(out=weight[:, c * S : (c + 1) * S], in_=wgt[:, c * S : (c + 1) * S])
         for i in range(1, PACK):
             nc.sync.dma_start(out=planes[i][:], in_=x_planes[:, i, :])
         for q in range(4):
@@ -56,71 +55,54 @@ def tile_list_hbag_tm_bias_kernel(tc, xT, w_words, w_scales, wgt, b, offs, out):
 
         bias_v = bias[:].rearrange("p (n h c) -> p h n c", h=2, c=4)
         for h in range(2):
-            spread = psum.tile([P, 4, P], F32, name=f"spread{h}")
+            spread = psum.tile([P, 4, P], F32, name=f"spread{h}", tag=f"bank{6 + h}")
             for c in range(4):
                 nc.tensor.transpose(spread[:, c, :], bcol[:, 4 * h + c : 4 * h + c + 1].to_broadcast([P, P]), ident[:])
             nc.scalar.copy(out=bias_v[:, h], in_=spread[:].rearrange("p c n -> p n c"))
 
-        low = keep.tile([P, 2, G * S], F32, name="low")
-        woven = {}
         codes = {q: keep.tile([P, CH], U32, name=f"codes{q}", align_bytes=64) for q in range(4)}
         scales = {q: keep.tile([P, CH], U8, name=f"scales{q}", align_bytes=64) for q in range(4)}
-        slots = {0: (6, 7), 1: (4, 6), 2: (5, 8), 3: (0, 5)}
 
-        def gather(i, q, count=1):
-            first = slots[q][i - 2]
+        def gather(dst, i, q, count=1):
             nc.vector.tensor_tensor(
-                arena[:, first : first + count, :].rearrange("p q c -> p (q c)"),
+                dst,
                 planes[i][:].indirect(offsets[:, q * (CH // 16) : (q + count) * (CH // 16)]),
-                arena[:, q : q + count, :].rearrange("p q c -> p (q c)"),
+                weight[:, q * CH : (q + count) * CH],
                 MULT,
             )
 
-        def weave_low(q):
-            woven[q] = keep.tile([P, CH, PACK], BF16, name=f"woven{q}", tag=f"woven{q // 2}", align_bytes=64)
-            nc.scalar.copy(out=woven[q][:, :, 0:2], in_=low[:, :, q * CH : (q + 1) * CH].rearrange("p t c -> p c t"))
+        def weave(dst, pair, src):
+            nc.scalar.copy(out=dst[:, :, 2 * pair : 2 * pair + 2], in_=src.rearrange("p t c -> p c t"))
 
-        def weave_high(q):
-            s2, s3 = slots[q]
-            nc.scalar.copy(out=woven[q][:, :, 2:4], in_=arena[:, s2 : s3 + 1 : s3 - s2, :].rearrange("p t c -> p c t"))
+        def quantise(q, src):
+            nc.vector.quantize_mx(out=codes[q][:].bitcast(FP8X4), scales=scales[q][:], in_=src.rearrange("p c t -> p (c t)"))
 
-        def quantise(q):
-            nc.vector.quantize_mx(
-                out=codes[q][:].bitcast(FP8X4),
-                scales=scales[q][:],
-                in_=woven[q][:].rearrange("p c t -> p (c t)"),
-            )
-
-        half = G * S // 2
+        low = keep.tile([P, 2, G * S], F32, name="low")
+        woven = keep.tile([P, 3 * CH, PACK], BF16, name="woven", tag="woven0", align_bytes=64)
+        high = {q: keep.tile([P, 2, CH], F32, name=f"high{q}", align_bytes=64) for q in range(3)}
+        part = {q: woven[:, q * CH : (q + 1) * CH, :] for q in range(3)}
         for c in range(G):
-            nc.vector.tensor_tensor(
-                low[:, 0, c * half : (c + 1) * half],
-                planes[0][:].indirect(offsets[:, c * half // 16 : (c + 1) * half // 16]),
-                arena[:, 2 * c : 2 * c + 2, :].rearrange("p q c -> p (q c)"),
-                MULT,
-            )
-        nc.vector.tensor_tensor(low[:, 1, :], planes[1][:].indirect(offsets[:]), arena[:, 0:4, :].rearrange("p q c -> p (q c)"), MULT)
-        weave_low(0)
-        weave_low(2)
-        gather(2, 0)
-        gather(2, 1, 2)
-        gather(3, 0)
-        gather(3, 2)
-        gather(2, 3)
-        weave_high(0)
-        quantise(0)
-        weave_high(2)
-        gather(3, 1)
-        quantise(2)
-        gather(3, 3)
-        weave_low(1)
-        weave_high(1)
-        quantise(1)
-        weave_low(3)
-        weave_high(3)
-        quantise(3)
+            gather(low[:, 0, c * S : (c + 1) * S], 0, 2 * c, 2)
+        gather(low[:, 1, :], 1, 0, 4)
+        weave(woven[:], 0, low[:, :, 0 : 3 * CH])
+        for i in range(2, PACK):
+            for q in (0, 2, 1):
+                gather(high[q][:, i - 2, :], i, q)
+        weave(part[0], 1, high[0][:])
+        quantise(0, part[0])
+        weave(part[2], 1, high[2][:])
+        high3 = keep.tile([P, 2, CH], F32, name="high3", tag="high0", align_bytes=64)
+        gather(high3[:, 0, :], 2, 3)
+        quantise(2, part[2])
+        gather(high3[:, 1, :], 3, 3)
+        weave(part[1], 1, high[1][:])
+        quantise(1, part[1])
+        woven3 = keep.tile([P, CH, PACK], BF16, name="woven3", tag="high2", align_bytes=64)
+        weave(woven3[:], 0, low[:, :, 3 * CH : 4 * CH])
+        weave(woven3[:], 1, high3[:])
+        quantise(3, woven3[:])
 
-        def product(acc, h, c, n0, width):
+        def product(acc, h, c, n0, width, start, stop):
             q = c * (S // CH) + h
             nc.tensor.matmul_mx(
                 out=acc,
@@ -128,8 +110,8 @@ def tile_list_hbag_tm_bias_kernel(tc, xT, w_words, w_scales, wgt, b, offs, out):
                 lhsT_scale=scales[q][:],
                 rhs=words[:, 2 * n0 : 2 * (n0 + width)].bitcast(FP4X4),
                 rhs_scale=wsc[:, n0 : n0 + width],
-                start=(c == 0),
-                stop=(c == G - 1),
+                start=start,
+                stop=stop,
             )
 
         def finish(acc, h, n0, width, queue):
@@ -137,17 +119,21 @@ def tile_list_hbag_tm_bias_kernel(tc, xT, w_words, w_scales, wgt, b, offs, out):
             nc.vector.tensor_tensor(res[:], acc[:], bias[:, n0 : n0 + width], ADD)
             queue.dma_start(out=out[h * CH : (h + 1) * CH, n0 : n0 + width], in_=res[:])
 
-        first = [psum.tile([P, NT], F32, name=f"first{n}") for n in range(2)]
-        for c in range(G):
-            for n in range(M // NT):
-                product(first[n][:], 0, c, n * NT, NT)
-        for n in range(M // NT):
-            finish(first[n], 0, n * NT, NT, nc.sync)
-        n0 = 0
-        for width, step, queue in ((512, 512, nc.sync), (256, 128, nc.sync), (128, 128, nc.scalar), (128, 128, nc.sync)):
-            acc = psum.tile([P, width], F32, name=f"second{n0}")
+        def passes(acc, h, c, n0, width):
+            step = NT if width == NT else CH
             for a in range(0, width, step):
-                for c in range(G):
-                    product(acc[:, a : a + step], 1, c, n0 + a, step)
-            finish(acc, 1, n0, width, queue)
-            n0 = n0 + width
+                product(acc[:, a : a + step], h, c, n0 + a, step, c == 0 and a == 0, c == G - 1 and a + step == width)
+
+        pieces = [(0, 0, 512), (0, 512, 256), (0, 768, 256), (1, 0, 256), (1, 256, 256), (1, 512, 256), (1, 768, 128), (1, 896, 128)]
+        acc = [psum.tile([P, width], F32, name=f"acc{j}", tag=f"bank{j}") for j, (h, n0, width) in enumerate(pieces)]
+        for c in range(G):
+            for j in range(2):
+                h, n0, width = pieces[j]
+                passes(acc[j], h, c, n0, width)
+        for j in range(2):
+            finish(acc[j], *pieces[j], nc.sync)
+        for j in range(2, len(pieces)):
+            h, n0, width = pieces[j]
+            for c in range(G):
+                passes(acc[j], h, c, n0, width)
+            finish(acc[j], h, n0, width, nc.scalar if j == 6 else nc.sync)

@@ -79,7 +79,9 @@ def tile_list_hbag_tm_bias_kernel(tc, xT, w_words, w_scales, wgt, b, offs, out):
 
         low = keep.tile([P, 2, G * S], F32, name="low")
         woven = keep.tile([P, 3 * CH, PACK], BF16, name="woven", tag="woven0", align_bytes=64)
-        high = {q: keep.tile([P, 2, CH], F32, name=f"high{q}", align_bytes=64) for q in range(3)}
+        shared = keep.tile([P, 4, CH], F32, name="shared")
+        high1 = keep.tile([P, 2, CH], F32, name="high1", align_bytes=64)
+        high = {0: shared[:, 0:2, :], 2: shared[:, 2:4, :], 1: high1[:], 3: shared[:, 1:3, :]}
         part = {q: woven[:, q * CH : (q + 1) * CH, :] for q in range(3)}
         for c in range(G):
             gather(low[:, 0, c * S : (c + 1) * S], 0, 2 * c, 2)
@@ -88,18 +90,17 @@ def tile_list_hbag_tm_bias_kernel(tc, xT, w_words, w_scales, wgt, b, offs, out):
         for i in range(2, PACK):
             for q in (0, 2, 1):
                 gather(high[q][:, i - 2, :], i, q)
-        weave(part[0], 1, high[0][:])
+        weave(part[0], 1, high[0])
         quantise(0, part[0])
-        weave(part[2], 1, high[2][:])
-        high3 = keep.tile([P, 2, CH], F32, name="high3", tag="high0", align_bytes=64)
-        gather(high3[:, 0, :], 2, 3)
+        weave(part[2], 1, high[2])
+        gather(high[3][:, 0, :], 2, 3)
         quantise(2, part[2])
-        gather(high3[:, 1, :], 3, 3)
-        weave(part[1], 1, high[1][:])
+        gather(high[3][:, 1, :], 3, 3)
+        weave(part[1], 1, high[1])
         quantise(1, part[1])
-        woven3 = keep.tile([P, CH, PACK], BF16, name="woven3", tag="high2", align_bytes=64)
+        woven3 = keep.tile([P, CH, PACK], BF16, name="woven3", tag="high1", align_bytes=64)
         weave(woven3[:], 0, low[:, :, 3 * CH : 4 * CH])
-        weave(woven3[:], 1, high3[:])
+        weave(woven3[:], 1, high[3])
         quantise(3, woven3[:])
 
         def product(acc, h, c, n0, width, start, stop):
@@ -114,26 +115,31 @@ def tile_list_hbag_tm_bias_kernel(tc, xT, w_words, w_scales, wgt, b, offs, out):
                 stop=stop,
             )
 
-        def finish(acc, h, n0, width, queue):
-            res = keep.tile([P, width], F32, name=f"res{h}_{n0}")
-            nc.vector.tensor_tensor(res[:], acc[:], bias[:, n0 : n0 + width], ADD)
-            queue.dma_start(out=out[h * CH : (h + 1) * CH, n0 : n0 + width], in_=res[:])
+        result = [keep.tile([P, M], F32, name=f"result{h}") for h in range(S // CH)]
+
+        def finish(acc, h, n0, width, stored, queue):
+            nc.vector.tensor_tensor(result[h][:, n0 : n0 + width], acc[:], bias[:, n0 : n0 + width], ADD)
+            if stored:
+                cols = slice(n0 + width - stored, n0 + width)
+                queue.dma_start(out=out[h * CH : (h + 1) * CH, cols], in_=result[h][:, cols])
 
         def passes(acc, h, c, n0, width):
             step = NT if width == NT else CH
             for a in range(0, width, step):
                 product(acc[:, a : a + step], h, c, n0 + a, step, c == 0 and a == 0, c == G - 1 and a + step == width)
 
-        pieces = [(0, 0, 512), (0, 512, 256), (0, 768, 256), (1, 0, 256), (1, 256, 256), (1, 512, 256), (1, 768, 128), (1, 896, 128)]
-        acc = [psum.tile([P, width], F32, name=f"acc{j}", tag=f"bank{j}") for j, (h, n0, width) in enumerate(pieces)]
+        pieces = [(0, 0, 256), (0, 256, 256), (0, 512, 256), (0, 768, 256), (1, 0, 256), (1, 256, 256), (1, 512, 256), (1, 768, 128), (1, 896, 128)]
+        stores = [0, 512, 256, 256, 256, 256, 256, 128, 128]
+        acc = {j: psum.tile([P, pieces[j][2]], F32, name=f"acc{j}", tag=f"bank{j}") for j in range(2)}
         for c in range(G):
             for j in range(2):
                 h, n0, width = pieces[j]
                 passes(acc[j], h, c, n0, width)
         for j in range(2):
-            finish(acc[j], *pieces[j], nc.sync)
+            finish(acc[j], *pieces[j], stores[j], nc.sync)
         for j in range(2, len(pieces)):
             h, n0, width = pieces[j]
+            acc[j] = psum.tile([P, width], F32, name=f"acc{j}", tag=f"bank{j % 8}")
             for c in range(G):
                 passes(acc[j], h, c, n0, width)
-            finish(acc[j], h, n0, width, nc.scalar if j == 6 else nc.sync)
+            finish(acc[j], h, n0, width, stores[j], nc.scalar if j == 7 else nc.sync)

@@ -51,7 +51,8 @@ def tile_list_hbag_tm_bias_kernel(tc, xT, w_words, w_scales, wgt, b, offs, out):
             nc.sync.dma_start(out=planes[i][:], in_=x_planes[:, i, :])
         for q in range(4):
             nc.sync.dma_start(out=wsc[32 * q : 32 * q + 4, :].bitcast(I32), in_=w_scales[0, 4 * q : 4 * q + 4, :].bitcast(I32))
-        nc.sync.dma_start(out=words[:].bitcast(I32), in_=w_words[0].bitcast(I32))
+        for n in range(2):
+            nc.sync.dma_start(out=words[:, n * M : (n + 1) * M].bitcast(I32), in_=w_words[0, :, n * M : (n + 1) * M].bitcast(I32))
 
         bias_v = bias[:].rearrange("p (n h c) -> p h n c", h=2, c=4)
         for h in range(2):
@@ -142,4 +143,4 @@ def tile_list_hbag_tm_bias_kernel(tc, xT, w_words, w_scales, wgt, b, offs, out):
             acc[j] = psum.tile([P, width], F32, name=f"acc{j}", tag=f"bank{j % 8}")
             for c in range(G):
                 passes(acc[j], h, c, n0, width)
-            finish(acc[j], h, n0, width, stores[j], nc.scalar if j == 7 else nc.sync)
+            finish(acc[j], h, n0, width, stores[j], nc.scalar if j % 2 == 1 else nc.sync)

from contextlib import ExitStack

import concourse.mybir as mybir
from concourse.masks import make_identity

G, K, M, T, S = 2, 512, 1024, 1024, 256
FLOPS = 2 * G * K * S * M

F32 = mybir.dt.float32
BF16 = mybir.dt.bfloat16
I32 = mybir.dt.int32
U32 = mybir.dt.uint32
U16 = mybir.dt.uint16
U8 = mybir.dt.uint8
FP8X4 = mybir.dt.float8_e4m3fn_x4
FP4X4 = mybir.dt.float4_e2m1fn_x4
MULT = mybir.AluOpType.mult
ADD = mybir.AluOpType.add

P = 128
PACK = 4
CH = 128
NT = 512


def tile_list_hbag_tm_bias_kernel(tc, xT, w_words, w_scales, wgt, b, offs, out):
    nc = tc.nc
    with ExitStack() as ctx:
        keep = ctx.enter_context(tc.tile_pool(name="keep", bufs=1))
        psum = ctx.enter_context(tc.psum_pool(name="psum", bufs=1))

        offsets = keep.tile([P, G * S // 16], U16, name="offsets")
        planes = [keep.tile([P, T], F32, name=f"plane{i}") for i in range(PACK)]
        weight = keep.tile([P, G * S], F32, name="weight")
        words = keep.tile([P, 2 * M], U8, name="words", align_bytes=64)
        wsc = keep.tile([P, M], U8, name="wsc", align_bytes=64)
        bcol = keep.tile([P, M // P], F32, name="bcol")
        ident = keep.tile([P, P], F32, name="ident", tag="woven0", align_bytes=64)
        bias = keep.tile([P, M], F32, name="bias")

        x_planes = xT.rearrange("(p i) t -> p i t", i=PACK)
        nc.scalar.dma_start(out=bcol[:], in_=b.rearrange("(p c) -> p c", p=P))
        nc.vector.memset(wsc[:].bitcast(I32), 0)
        make_identity(nc, ident[:])

        nc.sync.dma_start(out=planes[0][:], in_=x_planes[:, 0, :])
        nc.sync.dma_start(offsets[:], offs)
        for c in range(G):
            nc.sync.dma_start(out=weight[:, c * S : (c + 1) * S], in_=wgt[:, c * S : (c + 1) * S])
        for i in range(1, PACK):
            nc.sync.dma_start(out=planes[i][:], in_=x_planes[:, i, :])
        for q in range(4):
            nc.sync.dma_start(out=wsc[32 * q : 32 * q + 4, :].bitcast(I32), in_=w_scales[0, 4 * q : 4 * q + 4, :].bitcast(I32))
        for n in range(2):
            nc.sync.dma_start(out=words[:, n * M : (n + 1) * M].bitcast(I32), in_=w_words[0, :, n * M : (n + 1) * M].bitcast(I32))

        bias_v = bias[:].rearrange("p (n h c) -> p h n c", h=2, c=4)
        for h in range(2):
            spread = psum.tile([P, 4, P], F32, name=f"spread{h}", tag=f"bank{6 + h}")
            for c in range(4):
                nc.tensor.transpose(spread[:, c, :], bcol[:, 4 * h + c : 4 * h + c + 1].to_broadcast([P, P]), ident[:])
            nc.scalar.copy(out=bias_v[:, h], in_=spread[:].rearrange("p c n -> p n c"))

        codes = {q: keep.tile([P, CH], U32, name=f"codes{q}", align_bytes=64) for q in range(4)}
        scales = {q: keep.tile([P, CH], U8, name=f"scales{q}", align_bytes=64) for q in range(4)}

        def gather(dst, i, q, count=1):
            nc.vector.tensor_tensor(
                dst,
                planes[i][:].indirect(offsets[:, q * (CH // 16) : (q + count) * (CH // 16)]),
                weight[:, q * CH : (q + count) * CH],
                MULT,
            )

        def weave(dst, pair, src):
            nc.scalar.copy(out=dst[:, :, 2 * pair : 2 * pair + 2], in_=src.rearrange("p t c -> p c t"))

        def quantise(q, src):
            nc.vector.quantize_mx(out=codes[q][:].bitcast(FP8X4), scales=scales[q][:], in_=src.rearrange("p c t -> p (c t)"))

        low = keep.tile([P, 2, G * S], F32, name="low")
        woven = keep.tile([P, 3 * CH, PACK], BF16, name="woven", tag="woven0", align_bytes=64)
        shared = keep.tile([P, 4, CH], F32, name="shared")
        high1 = keep.tile([P, 2, CH], F32, name="high1", align_bytes=64)
        high = {0: shared[:, 0:2, :], 2: shared[:, 2:4, :], 1: high1[:], 3: shared[:, 1:3, :]}
        part = {q: woven[:, q * CH : (q + 1) * CH, :] for q in range(3)}
        for c in range(G):
            gather(low[:, 0, c * S : (c + 1) * S], 0, 2 * c, 2)
        gather(low[:, 1, :], 1, 0, 4)
        weave(woven[:], 0, low[:, :, 0 : 3 * CH])
        for i in range(2, PACK):
            for q in (0, 2, 1):
                gather(high[q][:, i - 2, :], i, q)
        weave(part[0], 1, high[0])
        quantise(0, part[0])
        weave(part[2], 1, high[2])
        gather(high[3][:, 0, :], 2, 3)
        quantise(2, part[2])
        gather(high[3][:, 1, :], 3, 3)
        weave(part[1], 1, high[1])
        quantise(1, part[1])
        woven3 = keep.tile([P, CH, PACK], BF16, name="woven3", tag="high1", align_bytes=64)
        weave(woven3[:], 0, low[:, :, 3 * CH : 4 * CH])
        weave(woven3[:], 1, high[3])
        quantise(3, woven3[:])

        def product(acc, h, c, n0, width, start, stop):
            q = c * (S // CH) + h
            nc.tensor.matmul_mx(
                out=acc,
                lhsT=codes[q][:].bitcast(FP8X4),
                lhsT_scale=scales[q][:],
                rhs=words[:, 2 * n0 : 2 * (n0 + width)].bitcast(FP4X4),
                rhs_scale=wsc[:, n0 : n0 + width],
                start=start,
                stop=stop,
            )

        result = [keep.tile([P, M], F32, name=f"result{h}") for h in range(S // CH)]

        def finish(acc, h, n0, width, stored, queue):
            nc.vector.tensor_tensor(result[h][:, n0 : n0 + width], acc[:], bias[:, n0 : n0 + width], ADD)
            if stored:
                cols = slice(n0 + width - stored, n0 + width)
                queue.dma_start(out=out[h * CH : (h + 1) * CH, cols], in_=result[h][:, cols])

        def passes(acc, h, c, n0, width):
            step = NT if width == NT else CH
            for a in range(0, width, step):
                product(acc[:, a : a + step], h, c, n0 + a, step, c == 0 and a == 0, c == G - 1 and a + step == width)

        pieces = [(0, 0, 256), (0, 256, 256), (0, 512, 256), (0, 768, 256), (1, 0, 256), (1, 256, 256), (1, 512, 256), (1, 768, 128), (1, 896, 128)]
        stores = [0, 512, 256, 256, 256, 256, 256, 128, 128]
        acc = {j: psum.tile([P, pieces[j][2]], F32, name=f"acc{j}", tag=f"bank{j}") for j in range(2)}
        for c in range(G):
            for j in range(2):
                h, n0, width = pieces[j]
                passes(acc[j], h, c, n0, width)
        for j in range(2):
            finish(acc[j], *pieces[j], stores[j], nc.sync)
        for j in range(2, len(pieces)):
            h, n0, width = pieces[j]
            acc[j] = psum.tile([P, width], F32, name=f"acc{j}", tag=f"bank{j % 8}")
            for c in range(G):
                passes(acc[j], h, c, n0, width)
            finish(acc[j], h, n0, width, stores[j], nc.scalar if j % 2 == 1 else nc.sync)
